import numpy as np
import ml_dtypes


def mxq(x, axis, fmt="e4m3"):
    dtype, down = {"e4m3": (ml_dtypes.float8_e4m3fn, 7), "e5m2": (ml_dtypes.float8_e5m2, 14)}[fmt]
    v = np.moveaxis(np.asarray(x, np.float32).astype(ml_dtypes.bfloat16).astype(np.float64), axis, -1)
    blocks = v.reshape(v.shape[:-1] + (-1, 32))
    amax = np.abs(blocks).max(-1, keepdims=True)
    byte = np.maximum(np.where(amax > 0, np.frexp(amax)[1] - 1 + 127, 0) - down, 1)
    scale = np.exp2(byte - 127.0)
    codes = (blocks / scale).astype(np.float32).astype(dtype).astype(np.float64)
    return np.moveaxis((codes * scale).reshape(v.shape), -1, axis)


WIDE = False


def mx_kscale(k):
    if not WIDE:
        return np.ones(k)
    levels = np.array([10, -10, 5, -5, 0])
    if k % 512:
        return np.exp2(np.random.permutation(np.resize(levels, k // 32))).repeat(32)
    a = np.empty((k // 512, 16))
    for p in range(k // 512):
        a[p, :8] = np.random.permutation(np.resize(levels, 8))
        for g in range(8):
            far = levels[np.abs(levels - a[p, g]) >= 10]
            a[p, g + 8] = far[np.random.randint(len(far))]
    return np.exp2(a.ravel()).repeat(32)


def f64(x):
    return np.asarray(x).astype(np.float64)


E2M1 = np.array([0.0, 0.5, 1.0, 1.5, 2.0, 3.0, 4.0, 6.0, -0.0, -0.5, -1.0, -1.5, -2.0, -3.0, -4.0, -6.0])


def pack_weight(w, fmt):
    k, n = w.shape
    w = f64(np.asarray(w, np.float32).astype(ml_dtypes.bfloat16)).reshape(k // 32, 32, n)
    amax = np.abs(w).max(1)
    if fmt == "e4m3":
        byte = np.frexp(amax)[1] - 1 + 127 - 7
    else:
        mant, ex = np.frexp(amax / 6.0)
        byte = np.where(mant > 0.5, ex, ex - 1) + 127
    byte = np.clip(np.where(amax > 0, byte, 1), 1, 254)
    scaled = (w * np.exp2(127.0 - byte)[:, None, :]).reshape(k, n).astype(np.float32)
    by_word = np.ascontiguousarray(scaled.reshape(k // 512, 128, 4, n).transpose(0, 1, 3, 2))
    if fmt == "e4m3":
        words = by_word.astype(ml_dtypes.float8_e4m3fn).view(np.uint8)
    else:
        c = by_word.astype(ml_dtypes.float4_e2m1fn).view(np.uint8) & 0xF
        words = (c[..., 0::2] | (c[..., 1::2] << 4)).reshape(k // 512, 128, 2 * n)
    return np.ascontiguousarray(words), np.ascontiguousarray(byte.astype(np.uint8).reshape(k // 512, 16, n))


def unpack_weight(words, scales, fmt):
    g, _, n = scales.shape
    words = np.ascontiguousarray(words).reshape(g, 128, n, -1)
    if fmt == "e4m3":
        vals = words.view(ml_dtypes.float8_e4m3fn).astype(np.float64)
    else:
        nib = np.empty((g, 128, n, 4), np.uint8)
        nib[..., 0::2] = words & 0xF
        nib[..., 1::2] = words >> 4
        vals = E2M1[nib]
    vals = vals * np.repeat(np.exp2(scales.astype(np.float64) - 127.0), 8, axis=1)[..., None]
    return vals.transpose(0, 1, 3, 2).reshape(g * 512, n)


def silu(v):
    return v / (1.0 + np.exp(-np.maximum(v, -700.0)))


O, K, M, T = 512, 1536, 1024, 1024


def setup_inputs():
    n = np.random.standard_normal
    s = mx_kscale(K)[:, None]
    x = n((K, T)); x[:O] *= 6.0
    w = n((K, M)) / np.sqrt(K) / s; w[:O] /= 2.0
    p_x4 = pack_weight(x[O:] * s[O:], "e2m1")
    p_w4 = pack_weight(w[O:], "e2m1")
    return {
        "x8": (x[:O] * s[:O]).astype(np.float32),
        "w8": (w[:O]).astype(np.float32),
        "x4_words": p_x4[0],
        "x4_scales": p_x4[1],
        "w4_words": p_w4[0],
        "w4_scales": p_w4[1],
        "b": (0.3 * n(1024)).astype(np.float32),
    }


def reference(x8, w8, x4_words, x4_scales, w4_words, w4_scales, b):
    x8_ = mxq(f64(x8), 0, "e4m3")
    w8_ = mxq(f64(w8), 0, "e4m3")
    x4_ = unpack_weight(x4_words, x4_scales, "e2m1")
    w4_ = unpack_weight(w4_words, w4_scales, "e2m1")
    y = x8_.T @ w8_ + x4_.T @ w4_
    return silu(y + f64(b)[None, :])

@@ -1,0 +1,233 @@
+from contextlib import ExitStack
+
+import concourse.mybir as mybir
+from concourse.masks import make_identity
+
+K8, K4, M, T = 512, 1024, 1024, 1024
+FLOPS = 2 * (K8 + K4) * M * T
+
+F32 = mybir.dt.float32
+BF16 = mybir.dt.bfloat16
+I32 = mybir.dt.int32
+U32 = mybir.dt.uint32
+U8 = mybir.dt.uint8
+FP8X4 = mybir.dt.float8_e4m3fn_x4
+FP4X4 = mybir.dt.float4_e2m1fn_x4
+SILU = mybir.ActivationFunctionType.Silu
+ADD = mybir.AluOpType.add
+
+P = 128
+PACK = 4
+HALF = 512
+XW = 256
+
+
+def tile_mix_atom_tm_silu_kernel(tc, x8, w8, x4_words, x4_scales, w4_words, w4_scales, b, out):
+    nc = tc.nc
+    with ExitStack() as ctx:
+        sb = ctx.enter_context(tc.tile_pool(name="sb", bufs=1))
+        psum = ctx.enter_context(tc.psum_pool(name="psum", bufs=8))
+        ctx.enter_context(tc.manual_schedule())
+
+        x8v = x8.rearrange("(p j) t -> p j t", j=PACK)
+        w8v = w8.rearrange("(p j) n -> p j n", j=PACK)
+        x4v = x4_words.rearrange("a p c -> p a c")
+        w4v = w4_words.rearrange("a p c -> p a c")
+
+        w_raw = [sb.tile([P, PACK, HALF], F32, name=f"w_raw{h}", tag=f"w_raw{h}") for h in range(2)]
+        x_raw = [sb.tile([P, PACK, XW], F32, name=f"x_raw{u}", tag=f"x_raw{u}") for u in range(4)]
+        w_grp = [sb.tile([P, HALF, PACK], BF16, name=f"w_grp{h}", tag=f"w_grp{h}", align_bytes=256) for h in range(2)]
+        x_grp = [sb.tile([P, XW, PACK], BF16, name=f"x_grp{u}", tag=f"x_grp{u}", align_bytes=256) for u in range(4)]
+        w_codes = [sb.tile([P, HALF], U32, name=f"w_codes{h}", tag=f"w_codes{h}", align_bytes=256) for h in range(2)]
+        w_sc = [sb.tile([P, HALF], U8, name=f"w_sc{h}", tag=f"w_sc{h}", align_bytes=256) for h in range(2)]
+        x_codes = [sb.tile([P, XW], U32, name=f"x_codes{u}", tag=f"x_codes{u}", align_bytes=256) for u in range(4)]
+        x_sc = [sb.tile([P, XW], U8, name=f"x_sc{u}", tag=f"x_sc{u}", align_bytes=256) for u in range(4)]
+        x4 = [sb.tile([P, 2, 1024], U8, name=f"x4w{h}", tag=f"x4w{h}", align_bytes=256) for h in range(2)]
+        w4 = [sb.tile([P, 2, 1024], U8, name=f"w4w{h}", tag=f"w4w{h}", align_bytes=256) for h in range(2)]
+        x4s = sb.tile([P, 2, 1024], U8, name="x4s", tag="x4s", align_bytes=256)
+        w4s = sb.tile([P, 2, 1024], U8, name="w4s", tag="w4s", align_bytes=256)
+        ident = sb.tile([P, P], F32, name="ident", tag="ident")
+        b_rows = sb.tile([P, P], F32, name="b_rows", tag="b_rows")
+        b_cols = sb.tile([P, 8], F32, name="b_cols", tag="b_cols")
+        bias = sb.tile([P, M], F32, name="bias", tag="bias")
+        warm = sb.tile([P, 8], F32, name="warm", tag="warm")
+
+        def as_i32(tile):
+            return tile[:].rearrange("p a c -> p (a c)").bitcast(I32)
+
+        def load_words(dst, view, h):
+            nc.sync.dma_start(
+                out=as_i32(dst).rearrange("p (a c) -> p a c", a=2),
+                in_=view.bitcast(I32)[:, :, 256 * h : 256 * (h + 1)],
+            )
+
+        def load_scales(engine, plane, scales, q):
+            engine.dma_start(
+                out=as_i32(plane)[32 * q : 32 * q + 4, :].rearrange("p (a c) -> p a c", a=2),
+                in_=scales.bitcast(I32)[:, 4 * q : 4 * q + 4, :].rearrange("a q c -> q a c"),
+            )
+
+        make_identity(nc, ident[:])
+        nc.vector.memset(b_rows[:], 0.0)
+        nc.vector.memset(as_i32(w4s), 0)
+        nc.vector.memset(as_i32(x4s), 0)
+        nc.vector.memset(warm[:], 0.0)
+
+        def load_w(h):
+            nc.sync.dma_start(out=w_raw[h][:], in_=w8v[:, :, HALF * h : HALF * (h + 1)])
+
+        def load_x(u):
+            nc.sync.dma_start(out=x_raw[u][:], in_=x8v[:, :, XW * u : XW * (u + 1)])
+
+        for q in range(4):
+            load_scales(nc.scalar, w4s, w4_scales, q)
+        nc.sync.dma_start(out=b_rows[0:8, :], in_=b.rearrange("(c f) -> c f", f=P))
+        load_w(0)
+        load_words(x4[0], x4v, 0)
+        load_words(w4[0], w4v, 0)
+        nc.scalar.activation(out=warm[:, 0:4], in_=warm[:, 4:8], func=SILU)
+        for q in range(4):
+            load_scales(nc.scalar, x4s, x4_scales, q)
+        load_x(0)
+        load_words(w4[1], w4v, 1)
+        load_x(1)
+        load_w(1)
+        load_words(x4[1], x4v, 1)
+        load_x(2)
+        load_x(3)
+
+        def copy(engine_copy, grp, raw, c0, c1):
+            engine_copy(
+                out=grp[:, c0:c1, :].rearrange("p (c i) t -> p c t i", i=4),
+                in_=raw[:, :, c0:c1].rearrange("p t (c i) -> p c t i", i=4),
+            )
+
+        def quant(codes, sc, grp, c0, c1):
+            nc.vector.quantize_mx(
+                out=codes[:, c0:c1].bitcast(FP8X4),
+                scales=sc[:, c0:c1],
+                in_=grp[:, c0:c1, :].rearrange("p c t -> p (c t)"),
+            )
+
+        def vx(u):
+            copy(nc.vector.tensor_copy, x_grp[u], x_raw[u], 0, 128)
+
+        def sx(u):
+            copy(nc.scalar.copy, x_grp[u], x_raw[u], 128, 256)
+
+        def qx(u, i):
+            quant(x_codes[u], x_sc[u], x_grp[u], 128 * i, 128 * (i + 1))
+
+        acc = {}
+        res = {}
+
+        def fp4(t, h):
+            bank = psum.tile([P, HALF], F32, name="bank", tag="bank")
+            acc[t, h] = bank
+            for a in range(2):
+                c = 128 * (t % 4)
+                nc.tensor.matmul_mx(
+                    out=bank[:],
+                    lhsT=x4[t // 4][:, a, 2 * c : 2 * c + 256].bitcast(FP4X4),
+                    lhsT_scale=x4s[:, a, 128 * t : 128 * (t + 1)],
+                    rhs=w4[h][:, a, :].bitcast(FP4X4),
+                    rhs_scale=w4s[:, a, HALF * h : HALF * (h + 1)],
+                    start=(a == 0),
+                    stop=False,
+                )
+
+        def fp8(t, h):
+            u, c = t // 2, 128 * (t % 2)
+            nc.tensor.matmul_mx(
+                out=acc[t, h][:],
+                lhsT=x_codes[u][:, c : c + 128].bitcast(FP8X4),
+                lhsT_scale=x_sc[u][:, c : c + 128],
+                rhs=w_codes[h][:].bitcast(FP8X4),
+                rhs_scale=w_sc[h][:],
+                start=False,
+                stop=True,
+            )
+
+        def add(t, h):
+            if h == 0:
+                res[t] = (
+                    sb.tile([P, M], F32, name=f"sum{t}", tag=f"sum{t}"),
+                    sb.tile([P, M], F32, name=f"res{t}", tag=f"res{t}"),
+                )
+            cols = slice(HALF * h, HALF * (h + 1))
+            nc.vector.tensor_tensor(out=res[t][0][:, cols], in0=acc[t, h][:], in1=bias[:, cols], op=ADD)
+
+        def silu(t, h):
+            cols = slice(HALF * h, HALF * (h + 1))
+            nc.scalar.activation(out=res[t][1][:, cols], in_=res[t][0][:, cols], func=SILU)
+
+        def store(t, c0, c1):
+            nc.sync.dma_start(out=out[128 * t : 128 * (t + 1), c0:c1], in_=res[t][1][:, c0:c1])
+
+        def store_half(t, h):
+            store(t, HALF * h, HALF * (h + 1))
+
+        bt = psum.tile([P, HALF], F32, name="bank", tag="bank")
+        nc.tensor.transpose(bt[:, 0:P], b_rows[:], ident[:])
+        nc.vector.tensor_copy(out=b_cols[:], in_=bt[:, 0:8])
+        for h in range(2):
+            bp = psum.tile([P, HALF], F32, name="bank", tag="bank")
+            for c in range(4):
+                nc.tensor.transpose(
+                    bp[:, P * c : P * (c + 1)], b_cols[:, 4 * h + c : 4 * h + c + 1].to_broadcast([P, P]), ident[:]
+                )
+            (nc.vector.tensor_copy if h == 0 else nc.scalar.copy)(out=bias[:, HALF * h : HALF * (h + 1)], in_=bp[:])
+
+        copy(nc.vector.tensor_copy, w_grp[0], w_raw[0], 0, 256)
+        copy(nc.scalar.copy, w_grp[0], w_raw[0], 256, 512)
+        quant(w_codes[0], w_sc[0], w_grp[0], 0, 256)
+        for t in range(4):
+            fp4(t, 0)
+        quant(w_codes[0], w_sc[0], w_grp[0], 256, 512)
+        vx(0); sx(0)
+        qx(0, 0)
+        fp8(0, 0)
+        qx(0, 1)
+        fp8(1, 0)
+        add(0, 0); silu(0, 0); store_half(0, 0)
+        fp4(0, 1); fp4(1, 1)
+        vx(1); sx(1)
+        add(1, 0); silu(1, 0); store_half(1, 0)
+        qx(1, 0); fp8(2, 0)
+        qx(1, 1); fp8(3, 0)
+        fp4(2, 1); fp4(3, 1)
+        add(2, 0); silu(2, 0); store_half(2, 0)
+        copy(nc.vector.tensor_copy, w_grp[1], w_raw[1], 0, 384)
+        copy(nc.scalar.copy, w_grp[1], w_raw[1], 384, 512)
+        add(3, 0); silu(3, 0); store_half(3, 0)
+        quant(w_codes[1], w_sc[1], w_grp[1], 0, 256)
+        quant(w_codes[1], w_sc[1], w_grp[1], 256, 512)
+        fp4(4, 0); fp4(4, 1); fp4(5, 0); fp4(5, 1)
+        for t in range(4):
+            fp8(t, 1)
+        add(0, 1); silu(0, 1); store_half(0, 1)
+        vx(2); sx(2)
+        add(1, 1); silu(1, 1); store_half(1, 1)
+        qx(2, 0)
+        fp4(6, 0)
+        fp8(4, 0); fp8(4, 1)
+        add(2, 1); silu(2, 1); store_half(2, 1)
+        qx(2, 1)
+        fp4(6, 1)
+        fp8(5, 0); fp8(5, 1)
+        add(3, 1); silu(3, 1); store_half(3, 1)
+        vx(3); sx(3)
+        add(4, 0); silu(4, 0)
+        qx(3, 0)
+        fp4(7, 0)
+        fp8(6, 0); fp8(6, 1)
+        add(4, 1); silu(4, 1); store(4, 0, M)
+        qx(3, 1)
+        fp4(7, 1)
+        fp8(7, 0); fp8(7, 1)
+        add(5, 0); silu(5, 0)
+        add(5, 1); silu(5, 1); store(5, 0, M)
+        add(6, 0); silu(6, 0)
+        add(6, 1); silu(6, 1); store(6, 0, M)
+        for h in range(2):
+            add(7, h); silu(7, h); store_half(7, h)

@@ -67,9 +67,9 @@ def tile_mix_atom_tm_silu_kernel(tc, x8, w8, x4_words, x4_scales, w4_words, w4_s
                 in_=scales.bitcast(I32)[:, 4 * q : 4 * q + 4, :].rearrange("a q c -> q a c"),
             )
 
-        make_identity(nc, ident[:])
-        nc.vector.memset(b_rows[:], 0.0)
         nc.vector.memset(as_i32(w4s), 0)
+        nc.gpsimd.memset(b_rows[:], 0.0)
+        make_identity(nc, ident[:])
         nc.vector.memset(as_i32(x4s), 0)
         nc.vector.memset(warm[:], 0.0)
 
@@ -79,22 +79,26 @@ def tile_mix_atom_tm_silu_kernel(tc, x8, w8, x4_words, x4_scales, w4_words, w4_s
         def load_x(u):
             nc.sync.dma_start(out=x_raw[u][:], in_=x8v[:, :, XW * u : XW * (u + 1)])
 
-        for q in range(4):
-            load_scales(nc.scalar, w4s, w4_scales, q)
-        nc.sync.dma_start(out=b_rows[0:8, :], in_=b.rearrange("(c f) -> c f", f=P))
-        load_w(0)
         load_words(x4[0], x4v, 0)
         load_words(w4[0], w4v, 0)
-        nc.scalar.activation(out=warm[:, 0:4], in_=warm[:, 4:8], func=SILU)
-        for q in range(4):
-            load_scales(nc.scalar, x4s, x4_scales, q)
+        nc.sync.dma_start(out=b_rows[0:8, :], in_=b.rearrange("(c f) -> c f", f=P))
+        load_scales(nc.sync, w4s, w4_scales, 0)
+        load_scales(nc.sync, w4s, w4_scales, 1)
+        load_scales(nc.sync, w4s, w4_scales, 2)
+        load_scales(nc.sync, w4s, w4_scales, 3)
+        load_w(0)
+        load_scales(nc.sync, x4s, x4_scales, 0)
+        load_scales(nc.sync, x4s, x4_scales, 1)
+        load_scales(nc.sync, x4s, x4_scales, 2)
+        load_scales(nc.sync, x4s, x4_scales, 3)
         load_x(0)
-        load_words(w4[1], w4v, 1)
         load_x(1)
+        load_words(w4[1], w4v, 1)
         load_w(1)
         load_words(x4[1], x4v, 1)
         load_x(2)
         load_x(3)
+        nc.scalar.activation(out=warm[:, 0:4], in_=warm[:, 4:8], func=SILU)
 
         def copy(engine_copy, grp, raw, c0, c1):
             engine_copy(
@@ -108,15 +112,6 @@ def tile_mix_atom_tm_silu_kernel(tc, x8, w8, x4_words, x4_scales, w4_words, w4_s
                 scales=sc[:, c0:c1],
                 in_=grp[:, c0:c1, :].rearrange("p c t -> p (c t)"),
             )
-
-        def vx(u):
-            copy(nc.vector.tensor_copy, x_grp[u], x_raw[u], 0, 128)
-
-        def sx(u):
-            copy(nc.scalar.copy, x_grp[u], x_raw[u], 128, 256)
-
-        def qx(u, i):
-            quant(x_codes[u], x_sc[u], x_grp[u], 128 * i, 128 * (i + 1))
 
         acc = {}
         res = {}
@@ -179,55 +174,84 @@ def tile_mix_atom_tm_silu_kernel(tc, x8, w8, x4_words, x4_scales, w4_words, w4_s
             (nc.vector.tensor_copy if h == 0 else nc.scalar.copy)(out=bias[:, HALF * h : HALF * (h + 1)], in_=bp[:])
 
         copy(nc.vector.tensor_copy, w_grp[0], w_raw[0], 0, 256)
+        copy(nc.vector.tensor_copy, x_grp[0], x_raw[0], 0, 128)
         copy(nc.scalar.copy, w_grp[0], w_raw[0], 256, 512)
-        quant(w_codes[0], w_sc[0], w_grp[0], 0, 256)
-        for t in range(4):
-            fp4(t, 0)
-        quant(w_codes[0], w_sc[0], w_grp[0], 256, 512)
-        vx(0); sx(0)
-        qx(0, 0)
+        copy(nc.scalar.copy, x_grp[0], x_raw[0], 128, 256)
+        copy(nc.scalar.copy, x_grp[1], x_raw[1], 128, 256)
+        fp4(0, 0)
+        fp4(1, 0)
+        fp4(2, 0)
+        quant(w_codes[0], w_sc[0], w_grp[0], 0, 512)
+        quant(x_codes[0], x_sc[0], x_grp[0], 0, 256)
+        copy(nc.vector.tensor_copy, x_grp[1], x_raw[1], 0, 128)
+        quant(x_codes[1], x_sc[1], x_grp[1], 0, 256)
         fp8(0, 0)
-        qx(0, 1)
         fp8(1, 0)
-        add(0, 0); silu(0, 0); store_half(0, 0)
-        fp4(0, 1); fp4(1, 1)
-        vx(1); sx(1)
-        add(1, 0); silu(1, 0); store_half(1, 0)
-        qx(1, 0); fp8(2, 0)
-        qx(1, 1); fp8(3, 0)
-        fp4(2, 1); fp4(3, 1)
-        add(2, 0); silu(2, 0); store_half(2, 0)
-        copy(nc.vector.tensor_copy, w_grp[1], w_raw[1], 0, 384)
-        copy(nc.scalar.copy, w_grp[1], w_raw[1], 384, 512)
-        add(3, 0); silu(3, 0); store_half(3, 0)
-        quant(w_codes[1], w_sc[1], w_grp[1], 0, 256)
-        quant(w_codes[1], w_sc[1], w_grp[1], 256, 512)
-        fp4(4, 0); fp4(4, 1); fp4(5, 0); fp4(5, 1)
-        for t in range(4):
-            fp8(t, 1)
-        add(0, 1); silu(0, 1); store_half(0, 1)
-        vx(2); sx(2)
-        add(1, 1); silu(1, 1); store_half(1, 1)
-        qx(2, 0)
+        fp4(3, 0)
+        fp8(2, 0)
+        fp8(3, 0)
+        fp4(0, 1)
+        fp4(1, 1)
+        fp4(2, 1)
+        fp4(3, 1)
+        add(0, 0)
+        add(1, 0)
+        add(2, 0)
+        copy(nc.vector.tensor_copy, w_grp[1], w_raw[1], 0, 256)
+        add(3, 0)
+        silu(0, 0); store_half(0, 0)
+        silu(1, 0); store_half(1, 0)
+        copy(nc.scalar.copy, w_grp[1], w_raw[1], 256, 512)
+        silu(2, 0); store_half(2, 0)
+        copy(nc.scalar.copy, x_grp[2], x_raw[2], 128, 256)
+        silu(3, 0); store_half(3, 0)
+        copy(nc.scalar.copy, x_grp[3], x_raw[3], 128, 256)
+        fp4(4, 0)
+        quant(w_codes[1], w_sc[1], w_grp[1], 0, 512)
+        copy(nc.vector.tensor_copy, x_grp[2], x_raw[2], 0, 128)
+        fp8(0, 1)
+        fp8(1, 1)
+        fp8(2, 1)
+        fp8(3, 1)
+        add(0, 1)
+        quant(x_codes[2], x_sc[2], x_grp[2], 0, 256)
+        copy(nc.vector.tensor_copy, x_grp[3], x_raw[3], 0, 128)
+        add(1, 1)
+        quant(x_codes[3], x_sc[3], x_grp[3], 0, 256)
+        add(2, 1)
+        add(3, 1)
+        silu(0, 1); store_half(0, 1)
+        silu(1, 1); store_half(1, 1)
+        silu(2, 1); store_half(2, 1)
+        silu(3, 1); store_half(3, 1)
+        fp8(4, 0)
+        fp4(4, 1)
+        fp8(4, 1)
+        fp4(5, 0)
+        fp8(5, 0)
+        fp4(5, 1)
+        fp8(5, 1)
         fp4(6, 0)
-        fp8(4, 0); fp8(4, 1)
-        add(2, 1); silu(2, 1); store_half(2, 1)
-        qx(2, 1)
+        fp8(6, 0)
         fp4(6, 1)
-        fp8(5, 0); fp8(5, 1)
-        add(3, 1); silu(3, 1); store_half(3, 1)
-        vx(3); sx(3)
-        add(4, 0); silu(4, 0)
-        qx(3, 0)
+        fp8(6, 1)
         fp4(7, 0)
-        fp8(6, 0); fp8(6, 1)
-        add(4, 1); silu(4, 1); store(4, 0, M)
-        qx(3, 1)
+        fp8(7, 0)
         fp4(7, 1)
-        fp8(7, 0); fp8(7, 1)
-        add(5, 0); silu(5, 0)
-        add(5, 1); silu(5, 1); store(5, 0, M)
-        add(6, 0); silu(6, 0)
-        add(6, 1); silu(6, 1); store(6, 0, M)
-        for h in range(2):
-            add(7, h); silu(7, h); store_half(7, h)
+        fp8(7, 1)
+        add(4, 0)
+        add(4, 1)
+        add(5, 0)
+        add(5, 1)
+        add(6, 0)
+        add(6, 1)
+        add(7, 0)
+        add(7, 1)
+        silu(4, 0)
+        silu(4, 1); store(4, 0, M)
+        silu(5, 0)
+        silu(5, 1); store(5, 0, M)
+        silu(6, 0)
+        silu(6, 1); store(6, 0, M)
+        silu(7, 0); store_half(7, 0)
+        silu(7, 1); store_half(7, 1)

from contextlib import ExitStack

import concourse.mybir as mybir
from concourse.masks import make_identity

K8, K4, M, T = 512, 1024, 1024, 1024
FLOPS = 2 * (K8 + K4) * M * T

F32 = mybir.dt.float32
BF16 = mybir.dt.bfloat16
I32 = mybir.dt.int32
U32 = mybir.dt.uint32
U8 = mybir.dt.uint8
FP8X4 = mybir.dt.float8_e4m3fn_x4
FP4X4 = mybir.dt.float4_e2m1fn_x4
SILU = mybir.ActivationFunctionType.Silu
ADD = mybir.AluOpType.add

P = 128
PACK = 4
HALF = 512
XW = 256


def tile_mix_atom_tm_silu_kernel(tc, x8, w8, x4_words, x4_scales, w4_words, w4_scales, b, out):
    nc = tc.nc
    with ExitStack() as ctx:
        sb = ctx.enter_context(tc.tile_pool(name="sb", bufs=1))
        psum = ctx.enter_context(tc.psum_pool(name="psum", bufs=8))
        ctx.enter_context(tc.manual_schedule())

        x8v = x8.rearrange("(p j) t -> p j t", j=PACK)
        w8v = w8.rearrange("(p j) n -> p j n", j=PACK)
        x4v = x4_words.rearrange("a p c -> p a c")
        w4v = w4_words.rearrange("a p c -> p a c")

        w_raw = [sb.tile([P, PACK, HALF], F32, name=f"w_raw{h}", tag=f"w_raw{h}") for h in range(2)]
        x_raw = [sb.tile([P, PACK, XW], F32, name=f"x_raw{u}", tag=f"x_raw{u}") for u in range(4)]
        w_grp = [sb.tile([P, HALF, PACK], BF16, name=f"w_grp{h}", tag=f"w_grp{h}", align_bytes=256) for h in range(2)]
        x_grp = [sb.tile([P, XW, PACK], BF16, name=f"x_grp{u}", tag=f"x_grp{u}", align_bytes=256) for u in range(4)]
        w_codes = [sb.tile([P, HALF], U32, name=f"w_codes{h}", tag=f"w_codes{h}", align_bytes=256) for h in range(2)]
        w_sc = [sb.tile([P, HALF], U8, name=f"w_sc{h}", tag=f"w_sc{h}", align_bytes=256) for h in range(2)]
        x_codes = [sb.tile([P, XW], U32, name=f"x_codes{u}", tag=f"x_codes{u}", align_bytes=256) for u in range(4)]
        x_sc = [sb.tile([P, XW], U8, name=f"x_sc{u}", tag=f"x_sc{u}", align_bytes=256) for u in range(4)]
        x4 = [sb.tile([P, 2, 1024], U8, name=f"x4w{h}", tag=f"x4w{h}", align_bytes=256) for h in range(2)]
        w4 = [sb.tile([P, 2, 1024], U8, name=f"w4w{h}", tag=f"w4w{h}", align_bytes=256) for h in range(2)]
        x4s = sb.tile([P, 2, 1024], U8, name="x4s", tag="x4s", align_bytes=256)
        w4s = sb.tile([P, 2, 1024], U8, name="w4s", tag="w4s", align_bytes=256)
        ident = sb.tile([P, P], F32, name="ident", tag="ident")
        b_rows = sb.tile([P, P], F32, name="b_rows", tag="b_rows")
        b_cols = sb.tile([P, 8], F32, name="b_cols", tag="b_cols")
        bias = sb.tile([P, M], F32, name="bias", tag="bias")
        warm = sb.tile([P, 8], F32, name="warm", tag="warm")

        def as_i32(tile):
            return tile[:].rearrange("p a c -> p (a c)").bitcast(I32)

        def load_words(dst, view, h):
            nc.sync.dma_start(
                out=as_i32(dst).rearrange("p (a c) -> p a c", a=2),
                in_=view.bitcast(I32)[:, :, 256 * h : 256 * (h + 1)],
            )

        def load_scales(engine, plane, scales, q):
            engine.dma_start(
                out=as_i32(plane)[32 * q : 32 * q + 4, :].rearrange("p (a c) -> p a c", a=2),
                in_=scales.bitcast(I32)[:, 4 * q : 4 * q + 4, :].rearrange("a q c -> q a c"),
            )

        nc.vector.memset(as_i32(w4s), 0)
        nc.gpsimd.memset(b_rows[:], 0.0)
        make_identity(nc, ident[:])
        nc.vector.memset(as_i32(x4s), 0)
        nc.vector.memset(warm[:], 0.0)

        def load_w(h):
            nc.sync.dma_start(out=w_raw[h][:], in_=w8v[:, :, HALF * h : HALF * (h + 1)])

        def load_x(u):
            nc.sync.dma_start(out=x_raw[u][:], in_=x8v[:, :, XW * u : XW * (u + 1)])

        load_words(x4[0], x4v, 0)
        load_words(w4[0], w4v, 0)
        nc.sync.dma_start(out=b_rows[0:8, :], in_=b.rearrange("(c f) -> c f", f=P))
        load_scales(nc.sync, w4s, w4_scales, 0)
        load_scales(nc.sync, w4s, w4_scales, 1)
        load_scales(nc.sync, w4s, w4_scales, 2)
        load_scales(nc.sync, w4s, w4_scales, 3)
        load_w(0)
        load_scales(nc.sync, x4s, x4_scales, 0)
        load_scales(nc.sync, x4s, x4_scales, 1)
        load_scales(nc.sync, x4s, x4_scales, 2)
        load_scales(nc.sync, x4s, x4_scales, 3)
        load_x(0)
        load_x(1)
        load_words(w4[1], w4v, 1)
        load_w(1)
        load_words(x4[1], x4v, 1)
        load_x(2)
        load_x(3)
        nc.scalar.activation(out=warm[:, 0:4], in_=warm[:, 4:8], func=SILU)

        def copy(engine_copy, grp, raw, c0, c1):
            engine_copy(
                out=grp[:, c0:c1, :].rearrange("p (c i) t -> p c t i", i=4),
                in_=raw[:, :, c0:c1].rearrange("p t (c i) -> p c t i", i=4),
            )

        def quant(codes, sc, grp, c0, c1):
            nc.vector.quantize_mx(
                out=codes[:, c0:c1].bitcast(FP8X4),
                scales=sc[:, c0:c1],
                in_=grp[:, c0:c1, :].rearrange("p c t -> p (c t)"),
            )

        acc = {}
        res = {}

        def fp4(t, h):
            bank = psum.tile([P, HALF], F32, name="bank", tag="bank")
            acc[t, h] = bank
            for a in range(2):
                c = 128 * (t % 4)
                nc.tensor.matmul_mx(
                    out=bank[:],
                    lhsT=x4[t // 4][:, a, 2 * c : 2 * c + 256].bitcast(FP4X4),
                    lhsT_scale=x4s[:, a, 128 * t : 128 * (t + 1)],
                    rhs=w4[h][:, a, :].bitcast(FP4X4),
                    rhs_scale=w4s[:, a, HALF * h : HALF * (h + 1)],
                    start=(a == 0),
                    stop=False,
                )

        def fp8(t, h):
            u, c = t // 2, 128 * (t % 2)
            nc.tensor.matmul_mx(
                out=acc[t, h][:],
                lhsT=x_codes[u][:, c : c + 128].bitcast(FP8X4),
                lhsT_scale=x_sc[u][:, c : c + 128],
                rhs=w_codes[h][:].bitcast(FP8X4),
                rhs_scale=w_sc[h][:],
                start=False,
                stop=True,
            )

        def add(t, h):
            if h == 0:
                res[t] = (
                    sb.tile([P, M], F32, name=f"sum{t}", tag=f"sum{t}"),
                    sb.tile([P, M], F32, name=f"res{t}", tag=f"res{t}"),
                )
            cols = slice(HALF * h, HALF * (h + 1))
            nc.vector.tensor_tensor(out=res[t][0][:, cols], in0=acc[t, h][:], in1=bias[:, cols], op=ADD)

        def silu(t, h):
            cols = slice(HALF * h, HALF * (h + 1))
            nc.scalar.activation(out=res[t][1][:, cols], in_=res[t][0][:, cols], func=SILU)

        def store(t, c0, c1):
            nc.sync.dma_start(out=out[128 * t : 128 * (t + 1), c0:c1], in_=res[t][1][:, c0:c1])

        def store_half(t, h):
            store(t, HALF * h, HALF * (h + 1))

        bt = psum.tile([P, HALF], F32, name="bank", tag="bank")
        nc.tensor.transpose(bt[:, 0:P], b_rows[:], ident[:])
        nc.vector.tensor_copy(out=b_cols[:], in_=bt[:, 0:8])
        for h in range(2):
            bp = psum.tile([P, HALF], F32, name="bank", tag="bank")
            for c in range(4):
                nc.tensor.transpose(
                    bp[:, P * c : P * (c + 1)], b_cols[:, 4 * h + c : 4 * h + c + 1].to_broadcast([P, P]), ident[:]
                )
            (nc.vector.tensor_copy if h == 0 else nc.scalar.copy)(out=bias[:, HALF * h : HALF * (h + 1)], in_=bp[:])

        copy(nc.vector.tensor_copy, w_grp[0], w_raw[0], 0, 256)
        copy(nc.vector.tensor_copy, x_grp[0], x_raw[0], 0, 128)
        copy(nc.scalar.copy, w_grp[0], w_raw[0], 256, 512)
        copy(nc.scalar.copy, x_grp[0], x_raw[0], 128, 256)
        copy(nc.scalar.copy, x_grp[1], x_raw[1], 128, 256)
        fp4(0, 0)
        fp4(1, 0)
        fp4(2, 0)
        quant(w_codes[0], w_sc[0], w_grp[0], 0, 512)
        quant(x_codes[0], x_sc[0], x_grp[0], 0, 256)
        copy(nc.vector.tensor_copy, x_grp[1], x_raw[1], 0, 128)
        quant(x_codes[1], x_sc[1], x_grp[1], 0, 256)
        fp8(0, 0)
        fp8(1, 0)
        fp4(3, 0)
        fp8(2, 0)
        fp8(3, 0)
        fp4(0, 1)
        fp4(1, 1)
        fp4(2, 1)
        fp4(3, 1)
        add(0, 0)
        add(1, 0)
        add(2, 0)
        copy(nc.vector.tensor_copy, w_grp[1], w_raw[1], 0, 256)
        add(3, 0)
        silu(0, 0); store_half(0, 0)
        silu(1, 0); store_half(1, 0)
        copy(nc.scalar.copy, w_grp[1], w_raw[1], 256, 512)
        silu(2, 0); store_half(2, 0)
        copy(nc.scalar.copy, x_grp[2], x_raw[2], 128, 256)
        silu(3, 0); store_half(3, 0)
        copy(nc.scalar.copy, x_grp[3], x_raw[3], 128, 256)
        fp4(4, 0)
        quant(w_codes[1], w_sc[1], w_grp[1], 0, 512)
        copy(nc.vector.tensor_copy, x_grp[2], x_raw[2], 0, 128)
        fp8(0, 1)
        fp8(1, 1)
        fp8(2, 1)
        fp8(3, 1)
        add(0, 1)
        quant(x_codes[2], x_sc[2], x_grp[2], 0, 256)
        copy(nc.vector.tensor_copy, x_grp[3], x_raw[3], 0, 128)
        add(1, 1)
        quant(x_codes[3], x_sc[3], x_grp[3], 0, 256)
        add(2, 1)
        add(3, 1)
        silu(0, 1); store_half(0, 1)
        silu(1, 1); store_half(1, 1)
        silu(2, 1); store_half(2, 1)
        silu(3, 1); store_half(3, 1)
        fp8(4, 0)
        fp4(4, 1)
        fp8(4, 1)
        fp4(5, 0)
        fp8(5, 0)
        fp4(5, 1)
        fp8(5, 1)
        fp4(6, 0)
        fp8(6, 0)
        fp4(6, 1)
        fp8(6, 1)
        fp4(7, 0)
        fp8(7, 0)
        fp4(7, 1)
        fp8(7, 1)
        add(4, 0)
        add(4, 1)
        add(5, 0)
        add(5, 1)
        add(6, 0)
        add(6, 1)
        add(7, 0)
        add(7, 1)
        silu(4, 0)
        silu(4, 1); store(4, 0, M)
        silu(5, 0)
        silu(5, 1); store(5, 0, M)
        silu(6, 0)
        silu(6, 1); store(6, 0, M)
        silu(7, 0); store_half(7, 0)
        silu(7, 1); store_half(7, 1)
